import numpy as np
import ml_dtypes


def mxq(x, axis, fmt="e4m3"):
    dtype, down = {"e4m3": (ml_dtypes.float8_e4m3fn, 7), "e5m2": (ml_dtypes.float8_e5m2, 14)}[fmt]
    v = np.moveaxis(np.asarray(x, np.float32).astype(ml_dtypes.bfloat16).astype(np.float64), axis, -1)
    blocks = v.reshape(v.shape[:-1] + (-1, 32))
    amax = np.abs(blocks).max(-1, keepdims=True)
    byte = np.maximum(np.where(amax > 0, np.frexp(amax)[1] - 1 + 127, 0) - down, 1)
    scale = np.exp2(byte - 127.0)
    codes = (blocks / scale).astype(np.float32).astype(dtype).astype(np.float64)
    return np.moveaxis((codes * scale).reshape(v.shape), -1, axis)


WIDE = False


def mx_kscale(k):
    if not WIDE:
        return np.ones(k)
    levels = np.array([10, -10, 5, -5, 0])
    if k % 512:
        return np.exp2(np.random.permutation(np.resize(levels, k // 32))).repeat(32)
    a = np.empty((k // 512, 16))
    for p in range(k // 512):
        a[p, :8] = np.random.permutation(np.resize(levels, 8))
        for g in range(8):
            far = levels[np.abs(levels - a[p, g]) >= 10]
            a[p, g + 8] = far[np.random.randint(len(far))]
    return np.exp2(a.ravel()).repeat(32)


def f64(x):
    return np.asarray(x).astype(np.float64)


def striped8(idx):
    return np.asarray(idx).reshape(8, -1, 16).transpose(0, 2, 1).reshape(128, -1).astype(np.uint16)


def unstriped8(offs):
    return offs.reshape(8, 16, -1).transpose(0, 2, 1).reshape(8, -1).astype(np.int64)


def pick8(x, idx, run):
    r = np.arange(len(x))
    return x[r[:, None], idx[r % (8 * run) // run]]


def sigmoid(v):
    return 1.0 / (1.0 + np.exp(-v))


D, T, I, Q, X, E = 512, 1024, 512, 256, 32, 512


def setup_inputs():
    n = np.random.standard_normal
    idx = np.stack([np.random.permutation(T)[:I] for _ in range(8)])
    fd = mx_kscale(D)
    fi = mx_kscale(I)
    ti = np.ones((8, T))
    np.put_along_axis(ti, idx, np.tile(fi, (8, 1)), axis=1)
    return {
        "query": (n((D, Q)) * (np.arange(D)[:, None] // 64 == np.arange(Q) % 8) * 0.0625 * fd[:, None]).astype(np.float32),
        "keys": (n((D, T)) / fd[:, None]).astype(np.float32),
        "size": (np.random.uniform(24.0, 64.0, (1, I)) * fi).astype(np.float32),
        "vals": (n((E, T)) / ti[np.arange(E) % 512 // 64]).astype(np.float32),
        "gval": (n((E, T)) / ti[np.arange(E) % 512 // 64]).astype(np.float32),
        "own": ((np.arange(E)[:, None] // 64 == np.arange(Q) % 8) * 1.0).astype(np.float32),
        "offs": striped8(idx),
    }


def reference(query, keys, size, vals, gval, own, offs):
    idx = unstriped8(offs)
    queryq = mxq(f64(query), 0, "e4m3")
    keysidxq = mxq(pick8(f64(keys), idx, 64), 0, "e4m3")
    a = queryq.T @ keysidxq
    p = np.exp(a - np.max(a, axis=1, keepdims=True))
    w = p * f64(size) / np.sum(p, axis=1, keepdims=True)
    wt = w.T
    vt = pick8(f64(vals), idx, 64).T
    vtq = mxq(vt, 0, "e4m3")
    wtq = mxq(wt, 0, "e4m3")
    o = vtq.T @ wtq
    ut = pick8(f64(gval), idx, 64).T
    utq = mxq(ut, 0, "e4m3")
    u = utq.T @ wtq
    ob = o * sigmoid(u) * f64(own)
    y = ob.reshape(E, X, Q // X).sum(axis=2)
    return y

@@ -1,0 +1,206 @@
+from contextlib import ExitStack
+
+import concourse.mybir as mybir
+from concourse.masks import make_identity
+
+D, T, I, Q, X, E = 512, 1024, 512, 256, 32, 512
+FLOPS = 2 * Q * D * I + 2 * 2 * E * I * Q
+
+F32 = mybir.dt.float32
+BF16 = mybir.dt.bfloat16
+U32 = mybir.dt.uint32
+U16 = mybir.dt.uint16
+U8 = mybir.dt.uint8
+FP8X4 = mybir.dt.float8_e4m3fn_x4
+ACT = mybir.ActivationFunctionType
+ALU = mybir.AluOpType
+AX = mybir.AxisListType
+
+P = 128
+PACK = 4
+LOADS = ["k00","k01","size","k10","k11","q","g0","v0","g1","own","v1","g2","v2","g3","v3"]
+ROAD = {"g0":"V","v0":"V","g1":"S","v1":"V","g2":"S","v2":"M","g3":"V","v3":"V"}
+KCAST = "SVSS"
+STEPS = ["c00","c01","k0","c10","c11","k1","Q","K","z","S","Gg0","Pg0","a0","Gv0","Pv0","f0","Gg1","Pg1","a1","Gv1","Pv1","f1","Gg2","Pg2","a2","Gv2","Pv2","f2","Gg3","Pg3","a3","Gv3","Pv3","f3"]
+
+
+def tile_attend_ownlists_valuegate_kernel(tc, query, keys, size, vals, gval, own, offs, out):
+    nc = tc.nc
+    with ExitStack() as ctx:
+        held = ctx.enter_context(tc.tile_pool(name="held", bufs=1))
+        psum = ctx.enter_context(tc.psum_pool(name="psum", bufs=1))
+
+        offsets = held.tile([P, I // 16], U16, name="offsets")
+        nc.sync.dma_start(offsets[:], offs)
+
+        warm = held.tile([P, 8], F32, name="warm")
+        nc.vector.memset(warm[:], 0.0)
+        warm_out = held.tile([P, 8], F32, name="warm_out")
+        nc.scalar.activation(warm_out[:], warm[:], ACT.Exp)
+
+        ident = held.tile([P, P], F32, name="ident")
+        make_identity(nc, ident[:])
+
+        keys4 = keys.rearrange("(p j) t -> p j t", j=PACK)
+        pools = {"v": vals.rearrange("(p j) t -> p j t", j=PACK), "g": gval.rearrange("(p j) t -> p j t", j=PACK)}
+        raw = {}
+        codes = {}
+        for name in LOADS:
+            if name == "q":
+                tile = held.tile([P, PACK, Q], F32, name="raw_q")
+                src = query.rearrange("(p j) q -> p j q", j=PACK)
+            elif name == "own":
+                tile = held.tile([P, PACK, Q], F32, name="raw_own")
+                src = own.rearrange("(p j) q -> p j q", j=PACK)
+            elif name == "size":
+                tile = held.tile([P, PACK], F32, name="raw_size")
+                src = size.rearrange("o (p j) -> (o p) j", j=PACK)
+            elif name[0] == "k":
+                u, h = int(name[1]), int(name[2])
+                tile = held.tile([P, 2, T // 2], F32, name="raw_" + name)
+                src = keys4[:, 2 * u : 2 * u + 2, h * (T // 2) : (h + 1) * (T // 2)]
+            else:
+                tile = held.tile([P, T], F32, name="raw_" + name)
+                src = pools[name[0]][:, int(name[1]), :]
+            nc.sync.dma_start(tile[:], src)
+            raw[name] = tile
+
+        def quantize(name, words, width):
+            code = held.tile([P, width], U32, name="code_" + name, align_bytes=64)
+            scale = held.tile([P, width], U8, name="scale_" + name, align_bytes=64)
+            nc.vector.quantize_mx(code[:].bitcast(FP8X4), scale[:], words)
+            codes[name] = (code, scale)
+
+        def product(dst, lhs, lhs_cols, rhs):
+            nc.tensor.matmul_mx(
+                dst,
+                lhsT=codes[lhs][0][:, lhs_cols].bitcast(FP8X4),
+                lhsT_scale=codes[lhs][1][:, lhs_cols],
+                rhs=codes[rhs][0][:].bitcast(FP8X4),
+                rhs_scale=codes[rhs][1][:],
+                start=True,
+                stop=True,
+            )
+
+        key_pairs = [held.tile([P, T], F32, name="key_pairs%d" % u) for u in range(2)]
+        key_listed = held.tile([P, 2, I], F32, name="key_listed")
+        size_bank = psum.tile([P, PACK, P], F32, name="size_bank")
+        result = held.tile([P, PACK, X], F32, name="result")
+        gates = {}
+
+        def cast_keys(u, h):
+            name = "k%d%d" % (u, h)
+            dst = key_pairs[u][:, h * (T // 2) : (h + 1) * (T // 2)].bitcast(BF16).rearrange("p (t e) -> p t e", e=2)
+            src = raw[name][:].rearrange("p e t -> p t e")
+            if KCAST[2 * u + h] == "S":
+                nc.scalar.activation(dst, src, ACT.Copy)
+            else:
+                nc.vector.tensor_copy(dst, src)
+
+        def gather_keys(u):
+            nc.vector.tensor_copy(key_listed[:, u, :], key_pairs[u][:].indirect(offsets[:]))
+
+        def pack_keys():
+            words = held.tile([P, I, 2], F32, name="key_words", align_bytes=64)
+            nc.scalar.copy(words[:], key_listed[:].rearrange("p u i -> p i u"))
+            quantize("k", words[:].rearrange("p i u -> p (i u)").bitcast(BF16), I)
+
+        def pack_query():
+            grouped = held.tile([P, Q, PACK], BF16, name="query_grouped", align_bytes=64)
+            nc.scalar.activation(grouped[:], raw["q"][:].rearrange("p j q -> p q j"), ACT.Copy)
+            quantize("q", grouped[:].rearrange("p q j -> p (q j)"), Q)
+
+        def spread_size():
+            for j in range(PACK):
+                nc.tensor.transpose(size_bank[:, j, :], raw["size"][:, j : j + 1].to_broadcast([P, P]), ident[:])
+
+        def softmax():
+            turned = psum.tile([P, 2, 2, P], F32, name="w_turned", tag="turn", bufs=3)
+            banks = [psum.tile([P, I], F32, name="scores%d" % a, tag="wide", bufs=2) for a in range(2)]
+            tops = [held.tile([P, 1], F32, name="top%d" % a) for a in range(2)]
+            sums = [held.tile([P, 1], F32, name="sum%d" % a) for a in range(2)]
+            invs = [held.tile([P, 1], F32, name="inv%d" % a) for a in range(2)]
+            exps = [held.tile([P, I], F32, name="exp%d" % a) for a in range(2)]
+            ws = [held.tile([P, I], BF16, name="w%d" % a) for a in range(2)]
+            for a in range(2):
+                product(banks[a][:], "q", slice(a * P, (a + 1) * P), "k")
+            for a in range(2):
+                nc.vector.tensor_reduce(tops[a][:], banks[a][:], AX.X, ALU.max, negate=True)
+                nc.scalar.activation(exps[a][:], banks[a][:], ACT.Exp, bias=tops[a][:], accum_out=sums[a][:])
+            for a in range(2):
+                nc.vector.reciprocal(invs[a][:], sums[a][:])
+            for a in range(2):
+                nc.vector.scalar_tensor_tensor(
+                    ws[a][:].rearrange("q (s j) -> q s j", j=PACK),
+                    exps[a][:].rearrange("q (s j) -> q s j", j=PACK),
+                    invs[a][:],
+                    size_bank[:].rearrange("q j s -> q s j"),
+                    ALU.mult,
+                    ALU.mult,
+                )
+                for u in range(2):
+                    nc.tensor.transpose(turned[:, a, u, :], ws[a][:].bitcast(F32)[:, u : I // 2 : 2], ident[:])
+            words = held.tile([P, 2, P, 2], F32, name="w_words", align_bytes=64)
+            nc.scalar.copy(words[:], turned[:].rearrange("s a u q -> s a q u"))
+            quantize("w", words[:].rearrange("s a q u -> s (a q u)").bitcast(BF16), Q)
+
+        listed = {}
+
+        def gather_plane(name):
+            listed[name] = held.tile([P, I], BF16, name="listed_" + name)
+            if ROAD[name] == "V":
+                nc.vector.tensor_copy(listed[name][:], raw[name][:].indirect(offsets[:]))
+            else:
+                rounded = held.tile([P, T], BF16, name="rounded_" + name)
+                if ROAD[name] == "S":
+                    nc.scalar.activation(rounded[:], raw[name][:], ACT.Copy)
+                else:
+                    nc.vector.tensor_copy(rounded[:], raw[name][:])
+                nc.scalar.activation(listed[name][:], rounded[:].indirect(offsets[:]), ACT.Copy)
+
+        def pack_plane(name):
+            turned = psum.tile([P, 2, P], F32, name="turned_" + name, tag="turn", bufs=3)
+            for u in range(2):
+                nc.tensor.transpose(turned[:, u, :], listed[name][:].bitcast(F32)[:, u : I // 2 : 2], ident[:])
+            words = held.tile([P, P, 2], F32, name="words_" + name, align_bytes=64)
+            nc.scalar.copy(words[:], turned[:].rearrange("s u p -> s p u"))
+            quantize(name, words[:].rearrange("s p u -> s (p u)").bitcast(BF16), P)
+
+        def gate(j):
+            bank = psum.tile([P, Q], F32, name="gate_sums%d" % j, tag="wide", bufs=2)
+            product(bank[:], "g%d" % j, slice(0, P), "w")
+            bent = held.tile([P, Q], F32, name="bent%d" % j)
+            nc.scalar.activation(bent[:], bank[:], ACT.Tanh, scale=0.5)
+            gates[j] = held.tile([P, Q], F32, name="gate%d" % j)
+            nc.vector.scalar_tensor_tensor(gates[j][:], bent[:], 1.0, raw["own"][:, j, :], ALU.add, ALU.mult)
+
+        def finish(j):
+            bank = psum.tile([P, Q], F32, name="value_sums%d" % j, tag="value", bufs=2)
+            product(bank[:], "v%d" % j, slice(0, P), "w")
+            gated = held.tile([P, Q], F32, name="gated%d" % j)
+            nc.vector.scalar_tensor_tensor(gated[:], bank[:], 0.5, gates[j][:], ALU.mult, ALU.mult)
+            nc.vector.tensor_reduce(result[:, j, :], gated[:].rearrange("p (x r) -> p x r", r=Q // X), AX.X, ALU.add)
+
+        for step in STEPS:
+            kind, arg = step[0], step[1:]
+            if kind == "c":
+                cast_keys(int(arg[0]), int(arg[1]))
+            elif kind == "k":
+                gather_keys(int(arg))
+            elif kind == "K":
+                pack_keys()
+            elif kind == "Q":
+                pack_query()
+            elif kind == "z":
+                spread_size()
+            elif kind == "S":
+                softmax()
+            elif kind == "G":
+                gather_plane(arg)
+            elif kind == "P":
+                pack_plane(arg)
+            elif kind == "a":
+                gate(int(arg))
+            else:
+                finish(int(arg))
+        nc.sync.dma_start(out.rearrange("(p j) x -> p j x", j=PACK), result[:])

@@ -14,193 +14,220 @@ U8 = mybir.dt.uint8
 FP8X4 = mybir.dt.float8_e4m3fn_x4
 ACT = mybir.ActivationFunctionType
 ALU = mybir.AluOpType
-AX = mybir.AxisListType
+AXIS = mybir.AxisListType
 
 P = 128
 PACK = 4
-LOADS = ["k00","k01","size","k10","k11","q","g0","v0","g1","own","v1","g2","v2","g3","v3"]
-ROAD = {"g0":"V","v0":"V","g1":"S","v1":"V","g2":"S","v2":"M","g3":"V","v3":"V"}
-KCAST = "SVSS"
-STEPS = ["c00","c01","k0","c10","c11","k1","Q","K","z","S","Gg0","Pg0","a0","Gv0","Pv0","f0","Gg1","Pg1","a1","Gv1","Pv1","f1","Gg2","Pg2","a2","Gv2","Pv2","f2","Gg3","Pg3","a3","Gv3","Pv3","f3"]
+ROW_TILES = Q // P
+SCALAR_TOKENS = 352
+SCALAR_GATES = 3
+TURN_BANKS = 3
 
 
 def tile_attend_ownlists_valuegate_kernel(tc, query, keys, size, vals, gval, own, offs, out):
     nc = tc.nc
     with ExitStack() as ctx:
-        held = ctx.enter_context(tc.tile_pool(name="held", bufs=1))
+        sbuf = ctx.enter_context(tc.tile_pool(name="sbuf", bufs=1))
         psum = ctx.enter_context(tc.psum_pool(name="psum", bufs=1))
 
-        offsets = held.tile([P, I // 16], U16, name="offsets")
+        def tile(name, shape, dtype, after=None):
+            return sbuf.tile(shape, dtype, name=name, tag=after or name, align_bytes=64)
+
+        def load(name, shape, src):
+            dst = tile(name, shape, F32)
+            nc.sync.dma_start(dst[:], src)
+            return dst
+
+        def planes(pool):
+            return pool.rearrange("(p j) c -> p j c", j=PACK)
+
+        key_rows = [load("key_rows0", [P, 2, T], planes(keys)[:, 0:2, :])]
+        offsets = sbuf.tile([P, I // 16], U16, name="offsets")
         nc.sync.dma_start(offsets[:], offs)
+        size_rows = load("size_rows", [P, PACK], size.rearrange("o (s j) -> (o s) j", j=PACK))
+        key_rows.append(load("key_rows1", [P, 2, T], planes(keys)[:, 2:4, :]))
+        query_rows = load("query_rows", [P, PACK, Q], planes(query))
+        pool_rows = {}
+        for j in range(PACK):
+            if j == PACK - 1:
+                own_rows = load("own_rows", [P, PACK, Q], planes(own))
+            pool_rows["gate", j] = load("gate_rows%d" % j, [P, T], planes(gval)[:, j, :])
+            pool_rows["value", j] = load("value_rows%d" % j, [P, T], planes(vals)[:, j, :])
 
-        warm = held.tile([P, 8], F32, name="warm")
-        nc.vector.memset(warm[:], 0.0)
-        warm_out = held.tile([P, 8], F32, name="warm_out")
-        nc.scalar.activation(warm_out[:], warm[:], ACT.Exp)
+        zeros = tile("zeros", [P, 8], F32)
+        nc.vector.memset(zeros[:], 0.0)
+        nc.scalar.activation(tile("warm", [P, 8], F32)[:], zeros[:], ACT.Exp)
+        identity = tile("identity", [P, P], F32)
+        make_identity(nc, identity[:])
 
-        ident = held.tile([P, P], F32, name="ident")
-        make_identity(nc, ident[:])
+        def quantize(name, grouped, columns, codes_after=None, scales_after=None):
+            codes = tile(name + "_codes", [P, columns], U32, codes_after)
+            scales = tile(name + "_scales", [P, columns], U8, scales_after)
+            nc.vector.quantize_mx(codes[:].bitcast(FP8X4), scales[:], grouped)
+            return codes, scales
 
-        keys4 = keys.rearrange("(p j) t -> p j t", j=PACK)
-        pools = {"v": vals.rearrange("(p j) t -> p j t", j=PACK), "g": gval.rearrange("(p j) t -> p j t", j=PACK)}
-        raw = {}
-        codes = {}
-        for name in LOADS:
-            if name == "q":
-                tile = held.tile([P, PACK, Q], F32, name="raw_q")
-                src = query.rearrange("(p j) q -> p j q", j=PACK)
-            elif name == "own":
-                tile = held.tile([P, PACK, Q], F32, name="raw_own")
-                src = own.rearrange("(p j) q -> p j q", j=PACK)
-            elif name == "size":
-                tile = held.tile([P, PACK], F32, name="raw_size")
-                src = size.rearrange("o (p j) -> (o p) j", j=PACK)
-            elif name[0] == "k":
-                u, h = int(name[1]), int(name[2])
-                tile = held.tile([P, 2, T // 2], F32, name="raw_" + name)
-                src = keys4[:, 2 * u : 2 * u + 2, h * (T // 2) : (h + 1) * (T // 2)]
-            else:
-                tile = held.tile([P, T], F32, name="raw_" + name)
-                src = pools[name[0]][:, int(name[1]), :]
-            nc.sync.dma_start(tile[:], src)
-            raw[name] = tile
-
-        def quantize(name, words, width):
-            code = held.tile([P, width], U32, name="code_" + name, align_bytes=64)
-            scale = held.tile([P, width], U8, name="scale_" + name, align_bytes=64)
-            nc.vector.quantize_mx(code[:].bitcast(FP8X4), scale[:], words)
-            codes[name] = (code, scale)
-
-        def product(dst, lhs, lhs_cols, rhs):
+        def product(dst, stationary, block, moving):
+            cols = slice(block * P, (block + 1) * P)
             nc.tensor.matmul_mx(
                 dst,
-                lhsT=codes[lhs][0][:, lhs_cols].bitcast(FP8X4),
-                lhsT_scale=codes[lhs][1][:, lhs_cols],
-                rhs=codes[rhs][0][:].bitcast(FP8X4),
-                rhs_scale=codes[rhs][1][:],
+                lhsT=stationary[0][:, cols].bitcast(FP8X4),
+                lhsT_scale=stationary[1][:, cols],
+                rhs=moving[0][:].bitcast(FP8X4),
+                rhs_scale=moving[1][:],
                 start=True,
                 stop=True,
             )
 
-        key_pairs = [held.tile([P, T], F32, name="key_pairs%d" % u) for u in range(2)]
-        key_listed = held.tile([P, 2, I], F32, name="key_listed")
-        size_bank = psum.tile([P, PACK, P], F32, name="size_bank")
-        result = held.tile([P, PACK, X], F32, name="result")
-        gates = {}
-
-        def cast_keys(u, h):
-            name = "k%d%d" % (u, h)
-            dst = key_pairs[u][:, h * (T // 2) : (h + 1) * (T // 2)].bitcast(BF16).rearrange("p (t e) -> p t e", e=2)
-            src = raw[name][:].rearrange("p e t -> p t e")
-            if KCAST[2 * u + h] == "S":
-                nc.scalar.activation(dst, src, ACT.Copy)
-            else:
-                nc.vector.tensor_copy(dst, src)
-
-        def gather_keys(u):
-            nc.vector.tensor_copy(key_listed[:, u, :], key_pairs[u][:].indirect(offsets[:]))
-
-        def pack_keys():
-            words = held.tile([P, I, 2], F32, name="key_words", align_bytes=64)
-            nc.scalar.copy(words[:], key_listed[:].rearrange("p u i -> p i u"))
-            quantize("k", words[:].rearrange("p i u -> p (i u)").bitcast(BF16), I)
-
-        def pack_query():
-            grouped = held.tile([P, Q, PACK], BF16, name="query_grouped", align_bytes=64)
-            nc.scalar.activation(grouped[:], raw["q"][:].rearrange("p j q -> p q j"), ACT.Copy)
-            quantize("q", grouped[:].rearrange("p q j -> p (q j)"), Q)
-
-        def spread_size():
-            for j in range(PACK):
-                nc.tensor.transpose(size_bank[:, j, :], raw["size"][:, j : j + 1].to_broadcast([P, P]), ident[:])
-
-        def softmax():
-            turned = psum.tile([P, 2, 2, P], F32, name="w_turned", tag="turn", bufs=3)
-            banks = [psum.tile([P, I], F32, name="scores%d" % a, tag="wide", bufs=2) for a in range(2)]
-            tops = [held.tile([P, 1], F32, name="top%d" % a) for a in range(2)]
-            sums = [held.tile([P, 1], F32, name="sum%d" % a) for a in range(2)]
-            invs = [held.tile([P, 1], F32, name="inv%d" % a) for a in range(2)]
-            exps = [held.tile([P, I], F32, name="exp%d" % a) for a in range(2)]
-            ws = [held.tile([P, I], BF16, name="w%d" % a) for a in range(2)]
-            for a in range(2):
-                product(banks[a][:], "q", slice(a * P, (a + 1) * P), "k")
-            for a in range(2):
-                nc.vector.tensor_reduce(tops[a][:], banks[a][:], AX.X, ALU.max, negate=True)
-                nc.scalar.activation(exps[a][:], banks[a][:], ACT.Exp, bias=tops[a][:], accum_out=sums[a][:])
-            for a in range(2):
-                nc.vector.reciprocal(invs[a][:], sums[a][:])
-            for a in range(2):
-                nc.vector.scalar_tensor_tensor(
-                    ws[a][:].rearrange("q (s j) -> q s j", j=PACK),
-                    exps[a][:].rearrange("q (s j) -> q s j", j=PACK),
-                    invs[a][:],
-                    size_bank[:].rearrange("q j s -> q s j"),
-                    ALU.mult,
-                    ALU.mult,
-                )
+        def turn(name, rows):
+            bank = psum.tile([P, len(rows), 2, P], F32, name=name, tag="turn", bufs=TURN_BANKS)
+            for n, row in enumerate(rows):
                 for u in range(2):
-                    nc.tensor.transpose(turned[:, a, u, :], ws[a][:].bitcast(F32)[:, u : I // 2 : 2], ident[:])
-            words = held.tile([P, 2, P, 2], F32, name="w_words", align_bytes=64)
-            nc.scalar.copy(words[:], turned[:].rearrange("s a u q -> s a q u"))
-            quantize("w", words[:].rearrange("s a q u -> s (a q u)").bitcast(BF16), Q)
+                    nc.tensor.transpose(bank[:, n, u, :], row.bitcast(F32)[:, u : I // 2 : 2], identity[:])
+            return bank
 
-        listed = {}
+        def unload(bank, words):
+            nc.scalar.copy(words, bank[:].rearrange("s n u c -> s n c u"))
 
-        def gather_plane(name):
-            listed[name] = held.tile([P, I], BF16, name="listed_" + name)
-            if ROAD[name] == "V":
-                nc.vector.tensor_copy(listed[name][:], raw[name][:].indirect(offsets[:]))
+        def grouped_view(words):
+            return words[:].rearrange("s n c u -> s (n c u)").bitcast(BF16)
+
+        rounded, listed = {}, {}
+
+        def round_gate(j):
+            rounded[j] = tile("gate_rounded%d" % j, [P, T], BF16)
+            nc.scalar.activation(rounded[j][:], pool_rows["gate", j][:], ACT.Copy)
+
+        def gather(kind, j):
+            listed[kind, j] = tile("%s_listed%d" % (kind, j), [P, I], BF16)
+            if kind == "gate" and j < SCALAR_GATES:
+                nc.scalar.activation(listed[kind, j][:], rounded[j][:].indirect(offsets[:]), ACT.Copy)
             else:
-                rounded = held.tile([P, T], BF16, name="rounded_" + name)
-                if ROAD[name] == "S":
-                    nc.scalar.activation(rounded[:], raw[name][:], ACT.Copy)
-                else:
-                    nc.vector.tensor_copy(rounded[:], raw[name][:])
-                nc.scalar.activation(listed[name][:], rounded[:].indirect(offsets[:]), ACT.Copy)
+                nc.vector.tensor_copy(listed[kind, j][:], pool_rows[kind, j][:].indirect(offsets[:]))
 
-        def pack_plane(name):
-            turned = psum.tile([P, 2, P], F32, name="turned_" + name, tag="turn", bufs=3)
-            for u in range(2):
-                nc.tensor.transpose(turned[:, u, :], listed[name][:].bitcast(F32)[:, u : I // 2 : 2], ident[:])
-            words = held.tile([P, P, 2], F32, name="words_" + name, align_bytes=64)
-            nc.scalar.copy(words[:], turned[:].rearrange("s u p -> s p u"))
-            quantize(name, words[:].rearrange("s p u -> s (p u)").bitcast(BF16), P)
+        def turn_planes(j, kinds=("gate", "value")):
+            return turn("turned_%s%d" % (kinds[0], j), [listed[kind, j][:] for kind in kinds])
+
+        size_bank = psum.tile([P, PACK, P], F32, name="size_bank")
+        for j in range(PACK):
+            nc.tensor.transpose(size_bank[:, j, :], size_rows[:, j : j + 1].to_broadcast([P, P]), identity[:])
+
+        key_listed = tile("key_listed", [P, 2, I], F32)
+        for u in range(2):
+            key_pairs = tile("key_pairs%d" % u, [P, T], F32)
+            halves = key_pairs[:].bitcast(BF16).rearrange("p (t e) -> p t e", e=2)
+            rows = key_rows[u][:].rearrange("p e t -> p t e")
+            nc.scalar.activation(halves[:, :SCALAR_TOKENS, :], rows[:, :SCALAR_TOKENS, :], ACT.Copy)
+            nc.vector.tensor_copy(halves[:, SCALAR_TOKENS:, :], rows[:, SCALAR_TOKENS:, :])
+            nc.vector.tensor_copy(key_listed[:, u, :], key_pairs[:].indirect(offsets[:]))
+        query_grouped = tile("query_grouped", [P, Q, PACK], BF16)
+        nc.scalar.activation(query_grouped[:], query_rows[:].rearrange("p j q -> p q j"), ACT.Copy)
+        key_words = tile("key_words", [P, I, 2], F32)
+        nc.vector.tensor_copy(key_words[:], key_listed[:].rearrange("p u i -> p i u"))
+        query_mx = quantize("query", query_grouped[:].rearrange("p q j -> p (q j)"), Q)
+        key_mx = quantize("key", key_words[:].rearrange("p i u -> p (i u)").bitcast(BF16), I)
+        scores = []
+        for a in range(ROW_TILES):
+            scores.append(psum.tile([P, I], F32, name="scores%d" % a, tag="wide", bufs=2))
+            product(scores[a][:], query_mx, a, key_mx)
+
+        round_gate(0)
+        gather("gate", 0)
+        gather("value", 0)
+        neg_max = tile("neg_max", [P, ROW_TILES], F32, after="gate_rounded0")
+        for a in range(ROW_TILES):
+            nc.vector.tensor_reduce(neg_max[:, a : a + 1], scores[a][:], AXIS.X, ALU.max, negate=True)
+        round_gate(1)
+        p = tile("p", [P, ROW_TILES, I], F32, after="gate_rows1")
+        row_sum = tile("row_sum", [P, ROW_TILES], F32)
+        for a in range(ROW_TILES):
+            nc.scalar.activation(
+                p[:, a, :], scores[a][:], ACT.Exp, bias=neg_max[:, a : a + 1], accum_out=row_sum[:, a : a + 1]
+            )
+        turned0 = turn_planes(0)
+        gather("value", 1)
+        inv_sum = tile("inv_sum", [P, ROW_TILES], F32)
+        nc.vector.reciprocal(inv_sum[:], row_sum[:])
+        w = [tile("w%d" % a, [P, I], BF16) for a in range(ROW_TILES)]
+        for a in range(ROW_TILES):
+            nc.vector.scalar_tensor_tensor(
+                w[a][:].rearrange("q (s j) -> q s j", j=PACK),
+                p[:, a, :].rearrange("q (s j) -> q s j", j=PACK),
+                inv_sum[:, a : a + 1],
+                size_bank[:].rearrange("q j s -> q s j"),
+                ALU.mult,
+                ALU.mult,
+            )
+        w_turned = turn("w_turned", [w[a][:] for a in range(ROW_TILES)])
+
+        gather("gate", 1)
+        words0 = tile("words0", [P, 2, P, 2], F32, after="gate_rounded0")
+        unload(turned0, words0[:])
+        round_gate(2)
+        w_words = tile("w_words", [P, ROW_TILES, P, 2], F32)
+        unload(w_turned, w_words[:])
+        gather("value", 2)
+        mx0 = quantize("planes0", grouped_view(words0), 2 * P)
+        turned1 = turn_planes(1)
+        gather("gate", 2)
+        gather("gate", 3)
+        words12 = tile("words12", [P, 4, P, 2], F32)
+        unload(turned1, words12[:, 0:2])
+        turned2 = turn_planes(2)
+        gather("value", 3)
+        gate_turned3 = turn_planes(3, ("gate",))
+        unload(turned2, words12[:, 2:4])
+        value_turned3 = turn_planes(3, ("value",))
+
+        w_mx = quantize("w", grouped_view(w_words), Q, codes_after="value_rows3")
+        words3 = tile("words3", [P, 2, P, 2], F32)
+        unload(gate_turned3, words3[:, 0:1])
+        unload(value_turned3, words3[:, 1:2])
+        mx12 = quantize("planes12", grouped_view(words12), 4 * P, scales_after="w_words")
+        operands = {0: (mx0, 0), 1: (mx12, 0), 2: (mx12, 2)}
+        tanh, sums = {}, {}
+
+        def gate_product(j):
+            bank = psum.tile([P, Q], F32, name="u%d" % j, tag="wide", bufs=2)
+            product(bank[:], operands[j][0], operands[j][1], w_mx)
+            return bank
+
+        def value_product(j):
+            sums[j] = psum.tile([P, Q], F32, name="o%d" % j, tag="value", bufs=2)
+            product(sums[j][:], operands[j][0], operands[j][1] + 1, w_mx)
+
+        def bend(j, bank):
+            tanh[j] = tile("tanh%d" % j, [P, Q], F32)
+            nc.scalar.activation(tanh[j][:], bank[:], ACT.Tanh, scale=0.5)
+
+        u0 = gate_product(0)
+        value_product(0)
+        bend(0, u0)
+        operands[3] = (quantize("planes3", grouped_view(words3), 2 * P), 0)
+        u1 = gate_product(1)
+        value_product(1)
+        bend(1, u1)
+        for j in (2, 3):
+            bend(j, gate_product(j))
+        for j in (2, 3):
+            value_product(j)
+
+        result = tile("result", [P, PACK, X], F32)
+        gates, gated = {}, {}
 
         def gate(j):
-            bank = psum.tile([P, Q], F32, name="gate_sums%d" % j, tag="wide", bufs=2)
-            product(bank[:], "g%d" % j, slice(0, P), "w")
-            bent = held.tile([P, Q], F32, name="bent%d" % j)
-            nc.scalar.activation(bent[:], bank[:], ACT.Tanh, scale=0.5)
-            gates[j] = held.tile([P, Q], F32, name="gate%d" % j)
-            nc.vector.scalar_tensor_tensor(gates[j][:], bent[:], 1.0, raw["own"][:, j, :], ALU.add, ALU.mult)
+            gates[j] = tile("gate%d" % j, [P, Q], F32)
+            nc.vector.scalar_tensor_tensor(gates[j][:], tanh[j][:], 1.0, own_rows[:, j, :], ALU.add, ALU.mult)
 
-        def finish(j):
-            bank = psum.tile([P, Q], F32, name="value_sums%d" % j, tag="value", bufs=2)
-            product(bank[:], "v%d" % j, slice(0, P), "w")
-            gated = held.tile([P, Q], F32, name="gated%d" % j)
-            nc.vector.scalar_tensor_tensor(gated[:], bank[:], 0.5, gates[j][:], ALU.mult, ALU.mult)
-            nc.vector.tensor_reduce(result[:, j, :], gated[:].rearrange("p (x r) -> p x r", r=Q // X), AX.X, ALU.add)
+        def apply_gate(j):
+            gated[j] = tile("gated%d" % j, [P, Q], F32)
+            nc.vector.scalar_tensor_tensor(gated[j][:], sums[j][:], 0.5, gates[j][:], ALU.mult, ALU.mult)
 
-        for step in STEPS:
-            kind, arg = step[0], step[1:]
-            if kind == "c":
-                cast_keys(int(arg[0]), int(arg[1]))
-            elif kind == "k":
-                gather_keys(int(arg))
-            elif kind == "K":
-                pack_keys()
-            elif kind == "Q":
-                pack_query()
-            elif kind == "z":
-                spread_size()
-            elif kind == "S":
-                softmax()
-            elif kind == "G":
-                gather_plane(arg)
-            elif kind == "P":
-                pack_plane(arg)
-            elif kind == "a":
-                gate(int(arg))
-            else:
-                finish(int(arg))
-        nc.sync.dma_start(out.rearrange("(p j) x -> p j x", j=PACK), result[:])
+        def add_heads(j):
+            nc.vector.tensor_reduce(
+                result[:, j, :], gated[j][:].rearrange("p (x r) -> p x r", r=Q // X), AXIS.X, ALU.add
+            )
+
+        for step, pair in ((gate, 0), (apply_gate, 0), (gate, 2), (add_heads, 0), (apply_gate, 2), (add_heads, 2)):
+            step(pair)
+            step(pair + 1)
+        nc.sync.dma_start(planes(out), result[:])

@@ -19,9 +19,10 @@ AXIS = mybir.AxisListType
 P = 128
 PACK = 4
 ROW_TILES = Q // P
+KINDS = ("gate", "value")
+RUN = 4
 SCALAR_TOKENS = 352
 SCALAR_GATES = 3
-TURN_BANKS = 3
 
 
 def tile_attend_ownlists_valuegate_kernel(tc, query, keys, size, vals, gval, own, offs, out):
@@ -60,9 +61,9 @@ def tile_attend_ownlists_valuegate_kernel(tc, query, keys, size, vals, gval, own
         identity = tile("identity", [P, P], F32)
         make_identity(nc, identity[:])
 
-        def quantize(name, grouped, columns, codes_after=None, scales_after=None):
+        def quantize(name, grouped, columns, codes_after=None):
             codes = tile(name + "_codes", [P, columns], U32, codes_after)
-            scales = tile(name + "_scales", [P, columns], U8, scales_after)
+            scales = tile(name + "_scales", [P, columns], U8)
             nc.vector.quantize_mx(codes[:].bitcast(FP8X4), scales[:], grouped)
             return codes, scales
 
@@ -72,18 +73,15 @@ def tile_attend_ownlists_valuegate_kernel(tc, query, keys, size, vals, gval, own
                 dst,
                 lhsT=stationary[0][:, cols].bitcast(FP8X4),
                 lhsT_scale=stationary[1][:, cols],
-                rhs=moving[0][:].bitcast(FP8X4),
-                rhs_scale=moving[1][:],
+                rhs=moving[0].bitcast(FP8X4),
+                rhs_scale=moving[1],
                 start=True,
                 stop=True,
             )
 
-        def turn(name, rows):
-            bank = psum.tile([P, len(rows), 2, P], F32, name=name, tag="turn", bufs=TURN_BANKS)
-            for n, row in enumerate(rows):
-                for u in range(2):
-                    nc.tensor.transpose(bank[:, n, u, :], row.bitcast(F32)[:, u : I // 2 : 2], identity[:])
-            return bank
+        def turn(row, dst):
+            for u in range(2):
+                nc.tensor.transpose(dst[:, u, :], row.bitcast(F32)[:, u : I // 2 : 2], identity[:])
 
         def unload(bank, words):
             nc.scalar.copy(words, bank[:].rearrange("s n u c -> s n c u"))
@@ -91,6 +89,7 @@ def tile_attend_ownlists_valuegate_kernel(tc, query, keys, size, vals, gval, own
         def grouped_view(words):
             return words[:].rearrange("s n c u -> s (n c u)").bitcast(BF16)
 
+        turned = [psum.tile([P, 2, 2, P], F32, name="turned%d" % j) for j in range(PACK)]
         rounded, listed = {}, {}
 
         def round_gate(j):
@@ -104,31 +103,39 @@ def tile_attend_ownlists_valuegate_kernel(tc, query, keys, size, vals, gval, own
             else:
                 nc.vector.tensor_copy(listed[kind, j][:], pool_rows[kind, j][:].indirect(offsets[:]))
 
-        def turn_planes(j, kinds=("gate", "value")):
-            return turn("turned_%s%d" % (kinds[0], j), [listed[kind, j][:] for kind in kinds])
+        def turn_plane(kind, j):
+            turn(listed[kind, j][:], turned[j][:, KINDS.index(kind)])
 
-        size_bank = psum.tile([P, PACK, P], F32, name="size_bank")
+        size_bank = psum.tile([P, PACK, P], F32, name="size_bank", tag="value", bufs=2)
         for j in range(PACK):
             nc.tensor.transpose(size_bank[:, j, :], size_rows[:, j : j + 1].to_broadcast([P, P]), identity[:])
 
         key_listed = tile("key_listed", [P, 2, I], F32)
         for u in range(2):
             key_pairs = tile("key_pairs%d" % u, [P, T], F32)
-            halves = key_pairs[:].bitcast(BF16).rearrange("p (t e) -> p t e", e=2)
-            rows = key_rows[u][:].rearrange("p e t -> p t e")
-            nc.scalar.activation(halves[:, :SCALAR_TOKENS, :], rows[:, :SCALAR_TOKENS, :], ACT.Copy)
-            nc.vector.tensor_copy(halves[:, SCALAR_TOKENS:, :], rows[:, SCALAR_TOKENS:, :])
+            halves = key_pairs[:].bitcast(BF16).rearrange("p (c r e) -> p c e r", r=RUN, e=2)
+            rows = key_rows[u][:].rearrange("p e (c r) -> p c e r", r=RUN)
+            split = SCALAR_TOKENS // RUN
+            nc.scalar.activation(halves[:, :split], rows[:, :split], ACT.Copy)
+            nc.vector.tensor_copy(halves[:, split:], rows[:, split:])
             nc.vector.tensor_copy(key_listed[:, u, :], key_pairs[:].indirect(offsets[:]))
         query_grouped = tile("query_grouped", [P, Q, PACK], BF16)
-        nc.scalar.activation(query_grouped[:], query_rows[:].rearrange("p j q -> p q j"), ACT.Copy)
+        nc.scalar.activation(
+            query_grouped[:].rearrange("p (c r) j -> p c j r", r=RUN),
+            query_rows[:].rearrange("p j (c r) -> p c j r", r=RUN),
+            ACT.Copy,
+        )
         key_words = tile("key_words", [P, I, 2], F32)
-        nc.vector.tensor_copy(key_words[:], key_listed[:].rearrange("p u i -> p i u"))
+        nc.vector.tensor_copy(
+            key_words[:].rearrange("p (c r) u -> p c u r", r=RUN),
+            key_listed[:].rearrange("p u (c r) -> p c u r", r=RUN),
+        )
         query_mx = quantize("query", query_grouped[:].rearrange("p q j -> p (q j)"), Q)
-        key_mx = quantize("key", key_words[:].rearrange("p i u -> p (i u)").bitcast(BF16), I)
+        key_mx = quantize("key", key_words[:].rearrange("p i u -> p (i u)").bitcast(BF16), I, codes_after="query_rows")
         scores = []
         for a in range(ROW_TILES):
             scores.append(psum.tile([P, I], F32, name="scores%d" % a, tag="wide", bufs=2))
-            product(scores[a][:], query_mx, a, key_mx)
+            product(scores[a][:], query_mx, a, (key_mx[0][:], key_mx[1][:]))
 
         round_gate(0)
         gather("gate", 0)
@@ -143,8 +150,10 @@ def tile_attend_ownlists_valuegate_kernel(tc, query, keys, size, vals, gval, own
             nc.scalar.activation(
                 p[:, a, :], scores[a][:], ACT.Exp, bias=neg_max[:, a : a + 1], accum_out=row_sum[:, a : a + 1]
             )
-        turned0 = turn_planes(0)
+        for kind in KINDS:
+            turn_plane(kind, 0)
         gather("value", 1)
+        turn_plane("value", 1)
         inv_sum = tile("inv_sum", [P, ROW_TILES], F32)
         nc.vector.reciprocal(inv_sum[:], row_sum[:])
         w = [tile("w%d" % a, [P, I], BF16) for a in range(ROW_TILES)]
@@ -157,59 +166,61 @@ def tile_attend_ownlists_valuegate_kernel(tc, query, keys, size, vals, gval, own
                 ALU.mult,
                 ALU.mult,
             )
-        w_turned = turn("w_turned", [w[a][:] for a in range(ROW_TILES)])
+        w_turned = psum.tile([P, ROW_TILES, 2, P], F32, name="w_turned", tag="wide", bufs=2)
+        for a in range(ROW_TILES):
+            turn(w[a][:], w_turned[:, a])
 
         gather("gate", 1)
-        words0 = tile("words0", [P, 2, P, 2], F32, after="gate_rounded0")
-        unload(turned0, words0[:])
+        turn_plane("gate", 1)
         round_gate(2)
-        w_words = tile("w_words", [P, ROW_TILES, P, 2], F32)
-        unload(w_turned, w_words[:])
-        gather("value", 2)
-        mx0 = quantize("planes0", grouped_view(words0), 2 * P)
-        turned1 = turn_planes(1)
-        gather("gate", 2)
+        for kind in ("value", "gate"):
+            gather(kind, 2)
+            turn_plane(kind, 2)
+        first_words = tile("first_words", [P, 4, P, 2], F32, after="gate_rounded2")
+        unload(w_turned, first_words[:, 0:2])
+        unload(turned[0], first_words[:, 2:4])
         gather("gate", 3)
-        words12 = tile("words12", [P, 4, P, 2], F32)
-        unload(turned1, words12[:, 0:2])
-        turned2 = turn_planes(2)
+        turn_plane("gate", 3)
+        middle_words = tile("middle_words", [P, 4, P, 2], F32, after="gate_listed2")
+        unload(turned[1], middle_words[:, 0:2])
+        unload(turned[2], middle_words[:, 2:4])
         gather("value", 3)
-        gate_turned3 = turn_planes(3, ("gate",))
-        unload(turned2, words12[:, 2:4])
-        value_turned3 = turn_planes(3, ("value",))
+        turn_plane("value", 3)
 
-        w_mx = quantize("w", grouped_view(w_words), Q, codes_after="value_rows3")
-        words3 = tile("words3", [P, 2, P, 2], F32)
-        unload(gate_turned3, words3[:, 0:1])
-        unload(value_turned3, words3[:, 1:2])
-        mx12 = quantize("planes12", grouped_view(words12), 4 * P, scales_after="w_words")
-        operands = {0: (mx0, 0), 1: (mx12, 0), 2: (mx12, 2)}
-        tanh, sums = {}, {}
+        first_mx = quantize("first", grouped_view(first_words), 4 * P, codes_after="value_rows3")
+        w_mx = (first_mx[0][:, 0:Q], first_mx[1][:, 0:Q])
+        operands = {0: (first_mx, ROW_TILES)}
+        gate_sums, tanh, sums = {}, {}, {}
 
         def gate_product(j):
-            bank = psum.tile([P, Q], F32, name="u%d" % j, tag="wide", bufs=2)
-            product(bank[:], operands[j][0], operands[j][1], w_mx)
-            return bank
+            gate_sums[j] = psum.tile([P, Q], F32, name="u%d" % j, tag="wide", bufs=2)
+            product(gate_sums[j][:], operands[j][0], operands[j][1], w_mx)
 
         def value_product(j):
             sums[j] = psum.tile([P, Q], F32, name="o%d" % j, tag="value", bufs=2)
             product(sums[j][:], operands[j][0], operands[j][1] + 1, w_mx)
 
-        def bend(j, bank):
+        def bend(j):
             tanh[j] = tile("tanh%d" % j, [P, Q], F32)
-            nc.scalar.activation(tanh[j][:], bank[:], ACT.Tanh, scale=0.5)
+            nc.scalar.activation(tanh[j][:], gate_sums[j][:], ACT.Tanh, scale=0.5)
 
-        u0 = gate_product(0)
+        gate_product(0)
         value_product(0)
-        bend(0, u0)
-        operands[3] = (quantize("planes3", grouped_view(words3), 2 * P), 0)
-        u1 = gate_product(1)
+        middle_mx = quantize("middle", grouped_view(middle_words), 4 * P, codes_after="gate_rounded2")
+        operands[1], operands[2] = (middle_mx, 0), (middle_mx, 2)
+        last_words = tile("last_words", [P, 2, P, 2], F32)
+        unload(turned[3], last_words[:])
+        bend(0)
+        gate_product(1)
+        gate_product(2)
         value_product(1)
-        bend(1, u1)
-        for j in (2, 3):
-            bend(j, gate_product(j))
-        for j in (2, 3):
-            value_product(j)
+        operands[3] = (quantize("last", grouped_view(last_words), 2 * P), 0)
+        bend(1)
+        bend(2)
+        gate_product(3)
+        value_product(2)
+        bend(3)
+        value_product(3)
 
         result = tile("result", [P, PACK, X], F32)
         gates, gated = {}, {}
@@ -227,7 +238,15 @@ def tile_attend_ownlists_valuegate_kernel(tc, query, keys, size, vals, gval, own
                 result[:, j, :], gated[j][:].rearrange("p (x r) -> p x r", r=Q // X), AXIS.X, ALU.add
             )
 
-        for step, pair in ((gate, 0), (apply_gate, 0), (gate, 2), (add_heads, 0), (apply_gate, 2), (add_heads, 2)):
-            step(pair)
-            step(pair + 1)
+        gate(0)
+        apply_gate(0)
+        gate(1)
+        add_heads(0)
+        apply_gate(1)
+        gate(2)
+        gate(3)
+        add_heads(1)
+        for step in (apply_gate, add_heads):
+            step(2)
+            step(3)
         nc.sync.dma_start(planes(out), result[:])

@@ -50,10 +50,9 @@ def tile_attend_ownlists_valuegate_kernel(tc, query, keys, size, vals, gval, own
         query_rows = load("query_rows", [P, PACK, Q], planes(query))
         pool_rows = {}
         for j in range(PACK):
-            if j == PACK - 1:
-                own_rows = load("own_rows", [P, PACK, Q], planes(own))
             pool_rows["gate", j] = load("gate_rows%d" % j, [P, T], planes(gval)[:, j, :])
             pool_rows["value", j] = load("value_rows%d" % j, [P, T], planes(vals)[:, j, :])
+        own_rows = load("own_rows", [P, PACK, Q], planes(own))
 
         zeros = tile("zeros", [P, 8], F32)
         nc.vector.memset(zeros[:], 0.0)

@@ -54,9 +54,6 @@ def tile_attend_ownlists_valuegate_kernel(tc, query, keys, size, vals, gval, own
             pool_rows["value", j] = load("value_rows%d" % j, [P, T], planes(vals)[:, j, :])
         own_rows = load("own_rows", [P, PACK, Q], planes(own))
 
-        zeros = tile("zeros", [P, 8], F32)
-        nc.vector.memset(zeros[:], 0.0)
-        nc.scalar.activation(tile("warm", [P, 8], F32)[:], zeros[:], ACT.Exp)
         identity = tile("identity", [P, P], F32)
         make_identity(nc, identity[:])
 
@@ -88,7 +85,7 @@ def tile_attend_ownlists_valuegate_kernel(tc, query, keys, size, vals, gval, own
         def grouped_view(words):
             return words[:].rearrange("s n c u -> s (n c u)").bitcast(BF16)
 
-        turned = [psum.tile([P, 2, 2, P], F32, name="turned%d" % j) for j in range(PACK)]
+        turned = [psum.tile([P, 2, 2, P], F32, name="turned%d" % j, tag="plane%d" % j) for j in range(PACK)]
         rounded, listed = {}, {}
 
         def round_gate(j):
@@ -192,11 +189,11 @@ def tile_attend_ownlists_valuegate_kernel(tc, query, keys, size, vals, gval, own
         gate_sums, tanh, sums = {}, {}, {}
 
         def gate_product(j):
-            gate_sums[j] = psum.tile([P, Q], F32, name="u%d" % j, tag="wide", bufs=2)
+            gate_sums[j] = psum.tile([P, Q], F32, name="u%d" % j, tag="plane%d" % j)
             product(gate_sums[j][:], operands[j][0], operands[j][1], w_mx)
 
         def value_product(j):
-            sums[j] = psum.tile([P, Q], F32, name="o%d" % j, tag="value", bufs=2)
+            sums[j] = psum.tile([P, Q], F32, name="o%d" % j, tag="value" if j < 2 else "wide", bufs=2)
             product(sums[j][:], operands[j][0], operands[j][1] + 1, w_mx)
 
         def bend(j):

from contextlib import ExitStack

import concourse.mybir as mybir
from concourse.masks import make_identity

D, T, I, Q, X, E = 512, 1024, 512, 256, 32, 512
FLOPS = 2 * Q * D * I + 2 * 2 * E * I * Q

F32 = mybir.dt.float32
BF16 = mybir.dt.bfloat16
U32 = mybir.dt.uint32
U16 = mybir.dt.uint16
U8 = mybir.dt.uint8
FP8X4 = mybir.dt.float8_e4m3fn_x4
ACT = mybir.ActivationFunctionType
ALU = mybir.AluOpType
AXIS = mybir.AxisListType

P = 128
PACK = 4
ROW_TILES = Q // P
KINDS = ("gate", "value")
RUN = 4
SCALAR_TOKENS = 352
SCALAR_GATES = 3


def tile_attend_ownlists_valuegate_kernel(tc, query, keys, size, vals, gval, own, offs, out):
    nc = tc.nc
    with ExitStack() as ctx:
        sbuf = ctx.enter_context(tc.tile_pool(name="sbuf", bufs=1))
        psum = ctx.enter_context(tc.psum_pool(name="psum", bufs=1))

        def tile(name, shape, dtype, after=None):
            return sbuf.tile(shape, dtype, name=name, tag=after or name, align_bytes=64)

        def load(name, shape, src):
            dst = tile(name, shape, F32)
            nc.sync.dma_start(dst[:], src)
            return dst

        def planes(pool):
            return pool.rearrange("(p j) c -> p j c", j=PACK)

        key_rows = [load("key_rows0", [P, 2, T], planes(keys)[:, 0:2, :])]
        offsets = sbuf.tile([P, I // 16], U16, name="offsets")
        nc.sync.dma_start(offsets[:], offs)
        size_rows = load("size_rows", [P, PACK], size.rearrange("o (s j) -> (o s) j", j=PACK))
        key_rows.append(load("key_rows1", [P, 2, T], planes(keys)[:, 2:4, :]))
        query_rows = load("query_rows", [P, PACK, Q], planes(query))
        pool_rows = {}
        for j in range(PACK):
            pool_rows["gate", j] = load("gate_rows%d" % j, [P, T], planes(gval)[:, j, :])
            pool_rows["value", j] = load("value_rows%d" % j, [P, T], planes(vals)[:, j, :])
        own_rows = load("own_rows", [P, PACK, Q], planes(own))

        identity = tile("identity", [P, P], F32)
        make_identity(nc, identity[:])

        def quantize(name, grouped, columns, codes_after=None):
            codes = tile(name + "_codes", [P, columns], U32, codes_after)
            scales = tile(name + "_scales", [P, columns], U8)
            nc.vector.quantize_mx(codes[:].bitcast(FP8X4), scales[:], grouped)
            return codes, scales

        def product(dst, stationary, block, moving):
            cols = slice(block * P, (block + 1) * P)
            nc.tensor.matmul_mx(
                dst,
                lhsT=stationary[0][:, cols].bitcast(FP8X4),
                lhsT_scale=stationary[1][:, cols],
                rhs=moving[0].bitcast(FP8X4),
                rhs_scale=moving[1],
                start=True,
                stop=True,
            )

        def turn(row, dst):
            for u in range(2):
                nc.tensor.transpose(dst[:, u, :], row.bitcast(F32)[:, u : I // 2 : 2], identity[:])

        def unload(bank, words):
            nc.scalar.copy(words, bank[:].rearrange("s n u c -> s n c u"))

        def grouped_view(words):
            return words[:].rearrange("s n c u -> s (n c u)").bitcast(BF16)

        turned = [psum.tile([P, 2, 2, P], F32, name="turned%d" % j, tag="plane%d" % j) for j in range(PACK)]
        rounded, listed = {}, {}

        def round_gate(j):
            rounded[j] = tile("gate_rounded%d" % j, [P, T], BF16)
            nc.scalar.activation(rounded[j][:], pool_rows["gate", j][:], ACT.Copy)

        def gather(kind, j):
            listed[kind, j] = tile("%s_listed%d" % (kind, j), [P, I], BF16)
            if kind == "gate" and j < SCALAR_GATES:
                nc.scalar.activation(listed[kind, j][:], rounded[j][:].indirect(offsets[:]), ACT.Copy)
            else:
                nc.vector.tensor_copy(listed[kind, j][:], pool_rows[kind, j][:].indirect(offsets[:]))

        def turn_plane(kind, j):
            turn(listed[kind, j][:], turned[j][:, KINDS.index(kind)])

        size_bank = psum.tile([P, PACK, P], F32, name="size_bank", tag="value", bufs=2)
        for j in range(PACK):
            nc.tensor.transpose(size_bank[:, j, :], size_rows[:, j : j + 1].to_broadcast([P, P]), identity[:])

        key_listed = tile("key_listed", [P, 2, I], F32)
        for u in range(2):
            key_pairs = tile("key_pairs%d" % u, [P, T], F32)
            halves = key_pairs[:].bitcast(BF16).rearrange("p (c r e) -> p c e r", r=RUN, e=2)
            rows = key_rows[u][:].rearrange("p e (c r) -> p c e r", r=RUN)
            split = SCALAR_TOKENS // RUN
            nc.scalar.activation(halves[:, :split], rows[:, :split], ACT.Copy)
            nc.vector.tensor_copy(halves[:, split:], rows[:, split:])
            nc.vector.tensor_copy(key_listed[:, u, :], key_pairs[:].indirect(offsets[:]))
        query_grouped = tile("query_grouped", [P, Q, PACK], BF16)
        nc.scalar.activation(
            query_grouped[:].rearrange("p (c r) j -> p c j r", r=RUN),
            query_rows[:].rearrange("p j (c r) -> p c j r", r=RUN),
            ACT.Copy,
        )
        key_words = tile("key_words", [P, I, 2], F32)
        nc.vector.tensor_copy(
            key_words[:].rearrange("p (c r) u -> p c u r", r=RUN),
            key_listed[:].rearrange("p u (c r) -> p c u r", r=RUN),
        )
        query_mx = quantize("query", query_grouped[:].rearrange("p q j -> p (q j)"), Q)
        key_mx = quantize("key", key_words[:].rearrange("p i u -> p (i u)").bitcast(BF16), I, codes_after="query_rows")
        scores = []
        for a in range(ROW_TILES):
            scores.append(psum.tile([P, I], F32, name="scores%d" % a, tag="wide", bufs=2))
            product(scores[a][:], query_mx, a, (key_mx[0][:], key_mx[1][:]))

        round_gate(0)
        gather("gate", 0)
        gather("value", 0)
        neg_max = tile("neg_max", [P, ROW_TILES], F32, after="gate_rounded0")
        for a in range(ROW_TILES):
            nc.vector.tensor_reduce(neg_max[:, a : a + 1], scores[a][:], AXIS.X, ALU.max, negate=True)
        round_gate(1)
        p = tile("p", [P, ROW_TILES, I], F32, after="gate_rows1")
        row_sum = tile("row_sum", [P, ROW_TILES], F32)
        for a in range(ROW_TILES):
            nc.scalar.activation(
                p[:, a, :], scores[a][:], ACT.Exp, bias=neg_max[:, a : a + 1], accum_out=row_sum[:, a : a + 1]
            )
        for kind in KINDS:
            turn_plane(kind, 0)
        gather("value", 1)
        turn_plane("value", 1)
        inv_sum = tile("inv_sum", [P, ROW_TILES], F32)
        nc.vector.reciprocal(inv_sum[:], row_sum[:])
        w = [tile("w%d" % a, [P, I], BF16) for a in range(ROW_TILES)]
        for a in range(ROW_TILES):
            nc.vector.scalar_tensor_tensor(
                w[a][:].rearrange("q (s j) -> q s j", j=PACK),
                p[:, a, :].rearrange("q (s j) -> q s j", j=PACK),
                inv_sum[:, a : a + 1],
                size_bank[:].rearrange("q j s -> q s j"),
                ALU.mult,
                ALU.mult,
            )
        w_turned = psum.tile([P, ROW_TILES, 2, P], F32, name="w_turned", tag="wide", bufs=2)
        for a in range(ROW_TILES):
            turn(w[a][:], w_turned[:, a])

        gather("gate", 1)
        turn_plane("gate", 1)
        round_gate(2)
        for kind in ("value", "gate"):
            gather(kind, 2)
            turn_plane(kind, 2)
        first_words = tile("first_words", [P, 4, P, 2], F32, after="gate_rounded2")
        unload(w_turned, first_words[:, 0:2])
        unload(turned[0], first_words[:, 2:4])
        gather("gate", 3)
        turn_plane("gate", 3)
        middle_words = tile("middle_words", [P, 4, P, 2], F32, after="gate_listed2")
        unload(turned[1], middle_words[:, 0:2])
        unload(turned[2], middle_words[:, 2:4])
        gather("value", 3)
        turn_plane("value", 3)

        first_mx = quantize("first", grouped_view(first_words), 4 * P, codes_after="value_rows3")
        w_mx = (first_mx[0][:, 0:Q], first_mx[1][:, 0:Q])
        operands = {0: (first_mx, ROW_TILES)}
        gate_sums, tanh, sums = {}, {}, {}

        def gate_product(j):
            gate_sums[j] = psum.tile([P, Q], F32, name="u%d" % j, tag="plane%d" % j)
            product(gate_sums[j][:], operands[j][0], operands[j][1], w_mx)

        def value_product(j):
            sums[j] = psum.tile([P, Q], F32, name="o%d" % j, tag="value" if j < 2 else "wide", bufs=2)
            product(sums[j][:], operands[j][0], operands[j][1] + 1, w_mx)

        def bend(j):
            tanh[j] = tile("tanh%d" % j, [P, Q], F32)
            nc.scalar.activation(tanh[j][:], gate_sums[j][:], ACT.Tanh, scale=0.5)

        gate_product(0)
        value_product(0)
        middle_mx = quantize("middle", grouped_view(middle_words), 4 * P, codes_after="gate_rounded2")
        operands[1], operands[2] = (middle_mx, 0), (middle_mx, 2)
        last_words = tile("last_words", [P, 2, P, 2], F32)
        unload(turned[3], last_words[:])
        bend(0)
        gate_product(1)
        gate_product(2)
        value_product(1)
        operands[3] = (quantize("last", grouped_view(last_words), 2 * P), 0)
        bend(1)
        bend(2)
        gate_product(3)
        value_product(2)
        bend(3)
        value_product(3)

        result = tile("result", [P, PACK, X], F32)
        gates, gated = {}, {}

        def gate(j):
            gates[j] = tile("gate%d" % j, [P, Q], F32)
            nc.vector.scalar_tensor_tensor(gates[j][:], tanh[j][:], 1.0, own_rows[:, j, :], ALU.add, ALU.mult)

        def apply_gate(j):
            gated[j] = tile("gated%d" % j, [P, Q], F32)
            nc.vector.scalar_tensor_tensor(gated[j][:], sums[j][:], 0.5, gates[j][:], ALU.mult, ALU.mult)

        def add_heads(j):
            nc.vector.tensor_reduce(
                result[:, j, :], gated[j][:].rearrange("p (x r) -> p x r", r=Q // X), AXIS.X, ALU.add
            )

        gate(0)
        apply_gate(0)
        gate(1)
        add_heads(0)
        apply_gate(1)
        gate(2)
        gate(3)
        add_heads(1)
        for step in (apply_gate, add_heads):
            step(2)
            step(3)
        nc.sync.dma_start(planes(out), result[:])
